import numpy as np
import ml_dtypes


def mxq(x, axis, fmt="e4m3"):
    dtype, down = {"e4m3": (ml_dtypes.float8_e4m3fn, 7), "e5m2": (ml_dtypes.float8_e5m2, 14)}[fmt]
    v = np.moveaxis(np.asarray(x, np.float32).astype(ml_dtypes.bfloat16).astype(np.float64), axis, -1)
    blocks = v.reshape(v.shape[:-1] + (-1, 32))
    amax = np.abs(blocks).max(-1, keepdims=True)
    byte = np.maximum(np.where(amax > 0, np.frexp(amax)[1] - 1 + 127, 0) - down, 1)
    scale = np.exp2(byte - 127.0)
    codes = (blocks / scale).astype(np.float32).astype(dtype).astype(np.float64)
    return np.moveaxis((codes * scale).reshape(v.shape), -1, axis)


WIDE = False


def mx_kscale(k):
    if not WIDE:
        return np.ones(k)
    levels = np.array([10, -10, 5, -5, 0])
    if k % 512:
        return np.exp2(np.random.permutation(np.resize(levels, k // 32))).repeat(32)
    a = np.empty((k // 512, 16))
    for p in range(k // 512):
        a[p, :8] = np.random.permutation(np.resize(levels, 8))
        for g in range(8):
            far = levels[np.abs(levels - a[p, g]) >= 10]
            a[p, g + 8] = far[np.random.randint(len(far))]
    return np.exp2(a.ravel()).repeat(32)


def f64(x):
    return np.asarray(x).astype(np.float64)


def striped(idx):
    return np.tile(np.asarray(idx).reshape(-1, 16).T, (8, 1)).astype(np.uint16)


def unstriped(offs):
    return offs[:16].T.reshape(-1).astype(np.int64)


E2M1 = np.array([0.0, 0.5, 1.0, 1.5, 2.0, 3.0, 4.0, 6.0, -0.0, -0.5, -1.0, -1.5, -2.0, -3.0, -4.0, -6.0])


def pack_weight(w, fmt):
    k, n = w.shape
    w = f64(np.asarray(w, np.float32).astype(ml_dtypes.bfloat16)).reshape(k // 32, 32, n)
    amax = np.abs(w).max(1)
    if fmt == "e4m3":
        byte = np.frexp(amax)[1] - 1 + 127 - 7
    else:
        mant, ex = np.frexp(amax / 6.0)
        byte = np.where(mant > 0.5, ex, ex - 1) + 127
    byte = np.clip(np.where(amax > 0, byte, 1), 1, 254)
    scaled = (w * np.exp2(127.0 - byte)[:, None, :]).reshape(k, n).astype(np.float32)
    by_word = np.ascontiguousarray(scaled.reshape(k // 512, 128, 4, n).transpose(0, 1, 3, 2))
    if fmt == "e4m3":
        words = by_word.astype(ml_dtypes.float8_e4m3fn).view(np.uint8)
    else:
        c = by_word.astype(ml_dtypes.float4_e2m1fn).view(np.uint8) & 0xF
        words = (c[..., 0::2] | (c[..., 1::2] << 4)).reshape(k // 512, 128, 2 * n)
    return np.ascontiguousarray(words), np.ascontiguousarray(byte.astype(np.uint8).reshape(k // 512, 16, n))


def unpack_weight(words, scales, fmt):
    g, _, n = scales.shape
    words = np.ascontiguousarray(words).reshape(g, 128, n, -1)
    if fmt == "e4m3":
        vals = words.view(ml_dtypes.float8_e4m3fn).astype(np.float64)
    else:
        nib = np.empty((g, 128, n, 4), np.uint8)
        nib[..., 0::2] = words & 0xF
        nib[..., 1::2] = words >> 4
        vals = E2M1[nib]
    vals = vals * np.repeat(np.exp2(scales.astype(np.float64) - 127.0), 8, axis=1)[..., None]
    return vals.transpose(0, 1, 3, 2).reshape(g * 512, n)


D, T, I, Q, E, Z = 512, 2048, 512, 128, 512, 1024


def setup_inputs():
    n = np.random.standard_normal
    idx = np.random.permutation(T)[:I]
    idx2 = np.random.permutation(Z)[:I]
    fd = mx_kscale(D)
    fi = mx_kscale(I)
    ti = np.ones(T)
    ti[idx] = fi
    keysp = pack_weight(n((D, T)) / fd[:, None], "e4m3")
    return {
        "query": (n((D, Q)) * 1.0 / np.sqrt(D) * fd[:, None]).astype(np.float32),
        "query2": (n((D, Q)) * 1.0 / np.sqrt(D) * fd[:, None]).astype(np.float32),
        "keys_words": keysp[0],
        "keys_scales": keysp[1],
        "pages": (n((D, Z)) / fd[:, None]).astype(np.float32),
        "os": (np.random.uniform(0.02, 0.08, (1, I)) * fi).astype(np.float32),
        "vals": (n((E, T)) / ti).astype(np.float32),
        "offs": striped(idx),
        "offs2": striped(idx2),
    }


def reference(query, query2, keys_words, keys_scales, pages, os, vals, offs, offs2):
    idx = unstriped(offs)
    idx2 = unstriped(offs2)
    keysu = unpack_weight(keys_words, keys_scales, "e4m3")
    queryq = mxq(f64(query), 0, "e4m3")
    keysidxg = keysu[:, idx]
    a = queryq.T @ keysidxg
    query2q = mxq(f64(query2), 0, "e4m3")
    pagesq = mxq(f64(pages), 0, "e4m3")
    h0 = query2q.T @ pagesq
    s = np.maximum(a, h0[:, idx2])
    w = np.maximum(s, 0.0)
    wo1 = w * f64(os)
    wt1 = wo1.T
    vt1 = f64(vals)[:, idx].T
    wt1q = mxq(wt1, 0, "e4m3")
    vt1q = mxq(vt1, 0, "e4m3")
    o = wt1q.T @ vt1q
    return o

@@ -1,0 +1,186 @@
+from contextlib import ExitStack
+
+import concourse.mybir as mybir
+from concourse.masks import make_identity
+
+D, T, I, Q, E, Z = 512, 2048, 512, 128, 512, 1024
+FLOPS = 2 * Q * (D * I + D * Z + I * E)
+
+F32 = mybir.dt.float32
+BF16 = mybir.dt.bfloat16
+I32 = mybir.dt.int32
+U32 = mybir.dt.uint32
+U16 = mybir.dt.uint16
+U8 = mybir.dt.uint8
+FP8X4 = mybir.dt.float8_e4m3fn_x4
+ALU = mybir.AluOpType
+COPY = mybir.ActivationFunctionType.Copy
+
+P = 128
+PACK = 4
+BANK = 512
+LIST_COLS = I // 16
+E_BLOCKS = E // P
+LAST_VECTOR_COLS = 16
+
+
+def interleave(copy, grouped, raw):
+    copy(
+        out=grouped.rearrange("p (c i) t -> p c t i", i=PACK),
+        in_=raw.rearrange("p t (c i) -> p c t i", i=PACK),
+    )
+
+
+def quantize(nc, codes, scales, grouped):
+    nc.vector.quantize_mx(out=codes.bitcast(FP8X4), scales=scales, in_=grouped.rearrange("p c t -> p (c t)"))
+
+
+def product(nc, acc, lhs_codes, lhs_scales, rhs_codes, rhs_scales):
+    nc.tensor.matmul_mx(
+        out=acc,
+        lhsT=lhs_codes.bitcast(FP8X4),
+        lhsT_scale=lhs_scales,
+        rhs=rhs_codes.bitcast(FP8X4),
+        rhs_scale=rhs_scales,
+        start=True,
+        stop=True,
+    )
+
+
+def tile_attend_widelarger_read_lean_kernel(tc, query, query2, keys_words, keys_scales, pages, factors, vals, offs, offs2, out):
+    nc = tc.nc
+    with ExitStack() as ctx:
+        sb = ctx.enter_context(tc.tile_pool(name="sb", bufs=1))
+        ps = ctx.enter_context(tc.psum_pool(name="ps", bufs=1))
+
+        token_list = sb.tile([P, LIST_COLS], U16)
+        page_list = sb.tile([P, LIST_COLS], U16)
+        pages_raw = sb.tile([P, PACK, Z], F32)
+        q2_raw = sb.tile([P, PACK, Q], F32)
+        q_raw = sb.tile([P, PACK, Q], F32)
+        slot_factor = sb.tile([P, PACK], F32)
+        key_words = sb.tile([P, T], U32)
+        key_bytes = sb.tile([P, T], U8)
+        vals_raw = [sb.tile([P, T], F32, name="vals_raw%d" % b, tag="vals_raw%d" % b, align_bytes=64) for b in range(E_BLOCKS)]
+        identity = sb.tile([P, P], F32)
+
+        nc.vector.memset(key_bytes[:].bitcast(I32), 0)
+        make_identity(nc, identity[:])
+
+        nc.sync.dma_start(out=pages_raw[:], in_=pages.rearrange("(p t) z -> p t z", t=PACK))
+        scale_rows = keys_scales[0].rearrange("(g j) c -> j g c", j=PACK)
+        for j in range(PACK):
+            nc.sync.dma_start(out=key_bytes[j:P:32, :].bitcast(I32), in_=scale_rows[j].bitcast(I32))
+        nc.sync.dma_start(out=q2_raw[:], in_=query2.rearrange("(p t) q -> p t q", t=PACK))
+        nc.sync.dma_start(out=q_raw[:], in_=query.rearrange("(p t) q -> p t q", t=PACK))
+        nc.sync.dma_start(
+            out=key_words[:].bitcast(I32), in_=keys_words[0].rearrange("p c r -> p (c r)").bitcast(I32)
+        )
+        nc.sync.dma_start(token_list[:], offs)
+        nc.sync.dma_start(page_list[:], offs2)
+        nc.sync.dma_start(out=slot_factor[:], in_=factors.rearrange("o (p t) -> p (o t)", t=PACK))
+        for b in range(E_BLOCKS):
+            nc.sync.dma_start(out=vals_raw[b][:], in_=vals[b * P : (b + 1) * P, :])
+
+        pg_codes = sb.tile([P, Z], U32, align_bytes=64)
+        pg_scales = sb.tile([P, Z], U8, align_bytes=64)
+        q2_codes = sb.tile([P, Q], U32, align_bytes=64)
+        q2_scales = sb.tile([P, Q], U8, align_bytes=64)
+        q_codes = sb.tile([P, Q], U32, align_bytes=64)
+        q_scales = sb.tile([P, Q], U8, align_bytes=64)
+        pg_a = sb.tile([P, 512, PACK], BF16, align_bytes=64)
+        pg_b = sb.tile([P, 256, PACK], BF16, align_bytes=64, tag="pg_b")
+        pg_c = sb.tile([P, 256, PACK], BF16, align_bytes=64, tag="pg_c")
+        q2_grouped = sb.tile([P, Q, PACK], BF16, align_bytes=64)
+        q_grouped = sb.tile([P, Q, PACK], BF16, align_bytes=64)
+
+        h0 = sb.tile([P, Z], F32, tag="h0", align_bytes=64)
+        h0_ps = [ps.tile([P, BANK], F32, name="h0_ps%d" % n, tag="bank%d" % n) for n in range(Z // BANK)]
+
+        interleave(nc.vector.tensor_copy, pg_a[:], pages_raw[:, :, 0:512])
+        interleave(nc.scalar.copy, pg_b[:], pages_raw[:, :, 512:768])
+        interleave(nc.scalar.copy, q2_grouped[:], q2_raw[:])
+        interleave(nc.scalar.copy, pg_c[:], pages_raw[:, :, 768:1024])
+        interleave(nc.scalar.copy, q_grouped[:], q_raw[:])
+        quantize(nc, pg_codes[:, 0:512], pg_scales[:, 0:512], pg_a[:])
+        quantize(nc, pg_codes[:, 512:768], pg_scales[:, 512:768], pg_b[:])
+        quantize(nc, q2_codes[:], q2_scales[:], q2_grouped[:])
+        quantize(nc, pg_codes[:, 768:1024], pg_scales[:, 768:1024], pg_c[:])
+        quantize(nc, q_codes[:], q_scales[:], q_grouped[:])
+        for n in range(Z // BANK):
+            cols = slice(n * BANK, (n + 1) * BANK)
+            product(nc, h0_ps[n][:], q2_codes[:], q2_scales[:], pg_codes[:, cols], pg_scales[:, cols])
+            nc.scalar.copy(out=h0[:, cols], in_=h0_ps[n][:])
+
+        picked_words = sb.tile([P, I], U32, align_bytes=64, tag="pg_c")
+        picked_bytes = sb.tile([P, I], U8, align_bytes=64, tag="pg_b")
+        nc.vector.tensor_copy(picked_words[:], key_words[:].indirect(token_list[:]))
+        nc.vector.tensor_copy(picked_bytes[:], key_bytes[:].indirect(token_list[:]))
+        a_ps = ps.tile([P, I], F32, tag="bank2")
+        product(nc, a_ps[:], q_codes[:], q_scales[:], picked_words[:], picked_bytes[:])
+
+        h0_picked = sb.tile([P, I], F32)
+        nc.scalar.activation(h0_picked[:], h0[:].indirect(page_list[:]), COPY)
+        weight = sb.tile([P, I], F32)
+        nc.vector.scalar_tensor_tensor(
+            out=weight[:], in0=a_ps[:], scalar=0.0, in1=h0_picked[:], op0=ALU.max, op1=ALU.max
+        )
+        wt_ps = ps.tile([P, PACK, Q], F32)
+        for t in range(PACK):
+            nc.tensor.transpose(wt_ps[:, t, :], weight[:, t:I:PACK], identity[:])
+        wt_grouped = sb.tile([P, Q, PACK], BF16, align_bytes=64)
+        nc.vector.tensor_tensor(
+            out=wt_grouped[:],
+            in0=wt_ps[:].rearrange("p t q -> p q t"),
+            in1=slot_factor[:].unsqueeze(1).to_broadcast([P, Q, PACK]),
+            op=ALU.mult,
+        )
+        wt_codes = sb.tile([P, Q], U32, align_bytes=64)
+        wt_scales = sb.tile([P, Q], U8, align_bytes=64)
+        quantize(nc, wt_codes[:], wt_scales[:], wt_grouped[:])
+
+        def gather(b, cut):
+            picked = sb.tile([P, I], BF16, name="picked%d" % b, tag=["h0", "picked1", "picked2", "picked2"][b], align_bytes=64)
+            if cut > 0:
+                nc.vector.tensor_copy(picked[:, : 16 * cut], vals_raw[b][:].indirect(token_list[:, :cut]))
+            nc.scalar.activation(picked[:, 16 * cut :], vals_raw[b][:].indirect(token_list[:, cut:]), COPY)
+            return picked
+
+        def turn(b, picked, copy):
+            pairs = picked[:].bitcast(F32)
+            vt_ps = ps.tile([P, 2, P], F32, name="vt_ps%d" % b, tag=["bank2", "bank4", "bank5", "bank6"][b])
+            for u in range(2):
+                nc.tensor.transpose(vt_ps[:, u, :], pairs[:, u : I // 2 : 2], identity[:])
+            vt_grouped = sb.tile([P, P, PACK], BF16, align_bytes=64, name="vt_grouped%d" % b, tag="vt_grouped%d" % b)
+            copy(out=vt_grouped[:].bitcast(F32), in_=vt_ps[:].rearrange("p u e -> p e u"))
+            return vt_grouped
+
+        v01_codes = sb.tile([P, 2 * P], U32, align_bytes=64)
+        v01_scales = sb.tile([P, 2 * P], U8, align_bytes=64)
+        for b in range(2):
+            grouped = turn(b, gather(b, 0), nc.vector.tensor_copy)
+            quantize(nc, v01_codes[:, b * P : (b + 1) * P], v01_scales[:, b * P : (b + 1) * P], grouped[:])
+        out01_ps = ps.tile([P, 2 * P], F32, tag="bank0")
+        product(nc, out01_ps[:], wt_codes[:], wt_scales[:], v01_codes[:], v01_scales[:])
+        grouped2 = turn(2, gather(2, 0), nc.vector.tensor_copy)
+        picked3 = gather(3, LAST_VECTOR_COLS)
+
+        head = sb.tile([P, 3 * P], F32, tag="vals_raw2", align_bytes=64)
+        v2_codes = sb.tile([P, P], U32, tag="vals_raw3", align_bytes=64)
+        v2_scales = sb.tile([P, P], U8, align_bytes=64)
+        quantize(nc, v2_codes[:], v2_scales[:], grouped2[:])
+        out2_ps = ps.tile([P, P], F32, tag="bank1")
+        product(nc, out2_ps[:], wt_codes[:], wt_scales[:], v2_codes[:], v2_scales[:])
+        nc.vector.tensor_copy(out=head[:, : 2 * P], in_=out01_ps[:])
+        nc.vector.tensor_copy(out=head[:, 2 * P :], in_=out2_ps[:])
+        nc.sync.dma_start(out=out[:, : 3 * P], in_=head[:])
+
+        grouped3 = turn(3, picked3, nc.scalar.copy)
+        v3_codes = sb.tile([P, P], U32, align_bytes=64)
+        v3_scales = sb.tile([P, P], U8, align_bytes=64)
+        quantize(nc, v3_codes[:], v3_scales[:], grouped3[:])
+        out3_ps = ps.tile([P, P], F32, tag="bank2")
+        product(nc, out3_ps[:], wt_codes[:], wt_scales[:], v3_codes[:], v3_scales[:])
+        tail = sb.tile([P, P], F32)
+        nc.scalar.copy(out=tail[:], in_=out3_ps[:])
+        nc.sync.dma_start(out=out[:, 3 * P :], in_=tail[:])

@@ -66,11 +66,11 @@ def tile_attend_widelarger_read_lean_kernel(tc, query, query2, keys_words, keys_
 
         nc.vector.memset(key_bytes[:].bitcast(I32), 0)
         make_identity(nc, identity[:])
-
-        nc.sync.dma_start(out=pages_raw[:], in_=pages.rearrange("(p t) z -> p t z", t=PACK))
         scale_rows = keys_scales[0].rearrange("(g j) c -> j g c", j=PACK)
         for j in range(PACK):
-            nc.sync.dma_start(out=key_bytes[j:P:32, :].bitcast(I32), in_=scale_rows[j].bitcast(I32))
+            nc.gpsimd.dma_start(out=key_bytes[j:P:32, :].bitcast(I32), in_=scale_rows[j].bitcast(I32))
+
+        nc.sync.dma_start(out=pages_raw[:], in_=pages.rearrange("(p t) z -> p t z", t=PACK))
         nc.sync.dma_start(out=q2_raw[:], in_=query2.rearrange("(p t) q -> p t q", t=PACK))
         nc.sync.dma_start(out=q_raw[:], in_=query.rearrange("(p t) q -> p t q", t=PACK))
         nc.sync.dma_start(

@@ -21,7 +21,7 @@ PACK = 4
 BANK = 512
 LIST_COLS = I // 16
 E_BLOCKS = E // P
-LAST_VECTOR_COLS = 16
+LAST_VECTOR_COLS = 18
 
 
 def interleave(copy, grouped, raw):
@@ -55,7 +55,7 @@ def tile_attend_widelarger_read_lean_kernel(tc, query, query2, keys_words, keys_
 
         token_list = sb.tile([P, LIST_COLS], U16)
         page_list = sb.tile([P, LIST_COLS], U16)
-        pages_raw = sb.tile([P, PACK, Z], F32)
+        pages_raw = [sb.tile([P, 2, Z], F32, name="pages_raw%d" % h) for h in range(2)]
         q2_raw = sb.tile([P, PACK, Q], F32)
         q_raw = sb.tile([P, PACK, Q], F32)
         slot_factor = sb.tile([P, PACK], F32)
@@ -64,19 +64,22 @@ def tile_attend_widelarger_read_lean_kernel(tc, query, query2, keys_words, keys_
         vals_raw = [sb.tile([P, T], F32, name="vals_raw%d" % b, tag="vals_raw%d" % b, align_bytes=64) for b in range(E_BLOCKS)]
         identity = sb.tile([P, P], F32)
 
-        nc.vector.memset(key_bytes[:].bitcast(I32), 0)
-        make_identity(nc, identity[:])
+        nc.gpsimd.memset(key_bytes[:].bitcast(I32), 0)
         scale_rows = keys_scales[0].rearrange("(g j) c -> j g c", j=PACK)
         for j in range(PACK):
             nc.gpsimd.dma_start(out=key_bytes[j:P:32, :].bitcast(I32), in_=scale_rows[j].bitcast(I32))
+        nc.vector.memset(identity[:], 0.0)
+        make_identity(nc, identity[:], nomemset=True)
 
-        nc.sync.dma_start(out=pages_raw[:], in_=pages.rearrange("(p t) z -> p t z", t=PACK))
+        page_rows = pages.rearrange("(p t) z -> p t z", t=PACK)
+        for h in range(2):
+            nc.sync.dma_start(out=pages_raw[h][:], in_=page_rows[:, 2 * h : 2 * h + 2, :])
+        nc.sync.dma_start(token_list[:], offs)
         nc.sync.dma_start(out=q2_raw[:], in_=query2.rearrange("(p t) q -> p t q", t=PACK))
         nc.sync.dma_start(out=q_raw[:], in_=query.rearrange("(p t) q -> p t q", t=PACK))
         nc.sync.dma_start(
             out=key_words[:].bitcast(I32), in_=keys_words[0].rearrange("p c r -> p (c r)").bitcast(I32)
         )
-        nc.sync.dma_start(token_list[:], offs)
         nc.sync.dma_start(page_list[:], offs2)
         nc.sync.dma_start(out=slot_factor[:], in_=factors.rearrange("o (p t) -> p (o t)", t=PACK))
         for b in range(E_BLOCKS):
@@ -88,34 +91,41 @@ def tile_attend_widelarger_read_lean_kernel(tc, query, query2, keys_words, keys_
         q2_scales = sb.tile([P, Q], U8, align_bytes=64)
         q_codes = sb.tile([P, Q], U32, align_bytes=64)
         q_scales = sb.tile([P, Q], U8, align_bytes=64)
-        pg_a = sb.tile([P, 512, PACK], BF16, align_bytes=64)
-        pg_b = sb.tile([P, 256, PACK], BF16, align_bytes=64, tag="pg_b")
-        pg_c = sb.tile([P, 256, PACK], BF16, align_bytes=64, tag="pg_c")
+        pg_a = sb.tile([P, 512, PACK], BF16, align_bytes=64, tag="pg_a")
+        pg_b = sb.tile([P, 512, PACK], BF16, align_bytes=64, tag="pg_b")
         q2_grouped = sb.tile([P, Q, PACK], BF16, align_bytes=64)
         q_grouped = sb.tile([P, Q, PACK], BF16, align_bytes=64)
 
         h0 = sb.tile([P, Z], F32, tag="h0", align_bytes=64)
         h0_ps = [ps.tile([P, BANK], F32, name="h0_ps%d" % n, tag="bank%d" % n) for n in range(Z // BANK)]
 
-        interleave(nc.vector.tensor_copy, pg_a[:], pages_raw[:, :, 0:512])
-        interleave(nc.scalar.copy, pg_b[:], pages_raw[:, :, 512:768])
+        def pair(copy, grouped, h, first, last):
+            base = first // BANK * BANK
+            copy(
+                out=grouped[:, first - base : last - base, 2 * h : 2 * h + 2],
+                in_=pages_raw[h][:, :, first:last].rearrange("p t z -> p z t"),
+            )
+
+        pair(nc.vector.tensor_copy, pg_a, 0, 0, 512)
+        pair(nc.vector.tensor_copy, pg_b, 0, 512, 1024)
+        pair(nc.vector.tensor_copy, pg_a, 1, 0, 512)
+        pair(nc.scalar.copy, pg_b, 1, 768, 1024)
+        pair(nc.vector.tensor_copy, pg_b, 1, 512, 768)
         interleave(nc.scalar.copy, q2_grouped[:], q2_raw[:])
-        interleave(nc.scalar.copy, pg_c[:], pages_raw[:, :, 768:1024])
         interleave(nc.scalar.copy, q_grouped[:], q_raw[:])
         quantize(nc, pg_codes[:, 0:512], pg_scales[:, 0:512], pg_a[:])
-        quantize(nc, pg_codes[:, 512:768], pg_scales[:, 512:768], pg_b[:])
         quantize(nc, q2_codes[:], q2_scales[:], q2_grouped[:])
-        quantize(nc, pg_codes[:, 768:1024], pg_scales[:, 768:1024], pg_c[:])
+        quantize(nc, pg_codes[:, 512:1024], pg_scales[:, 512:1024], pg_b[:])
         quantize(nc, q_codes[:], q_scales[:], q_grouped[:])
         for n in range(Z // BANK):
             cols = slice(n * BANK, (n + 1) * BANK)
             product(nc, h0_ps[n][:], q2_codes[:], q2_scales[:], pg_codes[:, cols], pg_scales[:, cols])
             nc.scalar.copy(out=h0[:, cols], in_=h0_ps[n][:])
 
-        picked_words = sb.tile([P, I], U32, align_bytes=64, tag="pg_c")
+        picked_words = sb.tile([P, I], U32, align_bytes=64, tag="pg_a")
         picked_bytes = sb.tile([P, I], U8, align_bytes=64, tag="pg_b")
-        nc.vector.tensor_copy(picked_words[:], key_words[:].indirect(token_list[:]))
         nc.vector.tensor_copy(picked_bytes[:], key_bytes[:].indirect(token_list[:]))
+        nc.vector.tensor_copy(picked_words[:], key_words[:].indirect(token_list[:]))
         a_ps = ps.tile([P, I], F32, tag="bank2")
         product(nc, a_ps[:], q_codes[:], q_scales[:], picked_words[:], picked_bytes[:])
 

@@ -150,7 +150,7 @@ def tile_attend_widelarger_read_lean_kernel(tc, query, query2, keys_words, keys_
         quantize(nc, wt_codes[:], wt_scales[:], wt_grouped[:])
 
         def gather(b, cut):
-            picked = sb.tile([P, I], BF16, name="picked%d" % b, tag=["h0", "picked1", "picked2", "picked2"][b], align_bytes=64)
+            picked = sb.tile([P, I], BF16, name="picked%d" % b, tag=["h0", "picked1", "picked2", "picked3"][b], align_bytes=64)
             if cut > 0:
                 nc.vector.tensor_copy(picked[:, : 16 * cut], vals_raw[b][:].indirect(token_list[:, :cut]))
             nc.scalar.activation(picked[:, 16 * cut :], vals_raw[b][:].indirect(token_list[:, cut:]), COPY)
@@ -161,7 +161,7 @@ def tile_attend_widelarger_read_lean_kernel(tc, query, query2, keys_words, keys_
             vt_ps = ps.tile([P, 2, P], F32, name="vt_ps%d" % b, tag=["bank2", "bank4", "bank5", "bank6"][b])
             for u in range(2):
                 nc.tensor.transpose(vt_ps[:, u, :], pairs[:, u : I // 2 : 2], identity[:])
-            vt_grouped = sb.tile([P, P, PACK], BF16, align_bytes=64, name="vt_grouped%d" % b, tag="vt_grouped%d" % b)
+            vt_grouped = sb.tile([P, P, PACK], BF16, align_bytes=64, name="vt_grouped%d" % b, tag=["vt0", "vt1", "vals_raw3", "vt3"][b])
             copy(out=vt_grouped[:].bitcast(F32), in_=vt_ps[:].rearrange("p u e -> p e u"))
             return vt_grouped
 
@@ -172,25 +172,19 @@ def tile_attend_widelarger_read_lean_kernel(tc, query, query2, keys_words, keys_
             quantize(nc, v01_codes[:, b * P : (b + 1) * P], v01_scales[:, b * P : (b + 1) * P], grouped[:])
         out01_ps = ps.tile([P, 2 * P], F32, tag="bank0")
         product(nc, out01_ps[:], wt_codes[:], wt_scales[:], v01_codes[:], v01_scales[:])
-        grouped2 = turn(2, gather(2, 0), nc.vector.tensor_copy)
+        head = sb.tile([P, 2 * P], F32)
+        nc.vector.tensor_copy(out=head[:], in_=out01_ps[:])
+        nc.sync.dma_start(out=out[:, : 2 * P], in_=head[:])
+        picked2 = gather(2, 0)
         picked3 = gather(3, LAST_VECTOR_COLS)
-
-        head = sb.tile([P, 3 * P], F32, tag="vals_raw2", align_bytes=64)
-        v2_codes = sb.tile([P, P], U32, tag="vals_raw3", align_bytes=64)
-        v2_scales = sb.tile([P, P], U8, align_bytes=64)
-        quantize(nc, v2_codes[:], v2_scales[:], grouped2[:])
-        out2_ps = ps.tile([P, P], F32, tag="bank1")
-        product(nc, out2_ps[:], wt_codes[:], wt_scales[:], v2_codes[:], v2_scales[:])
-        nc.vector.tensor_copy(out=head[:, : 2 * P], in_=out01_ps[:])
-        nc.vector.tensor_copy(out=head[:, 2 * P :], in_=out2_ps[:])
-        nc.sync.dma_start(out=out[:, : 3 * P], in_=head[:])
-
+        grouped2 = turn(2, picked2, nc.scalar.copy)
         grouped3 = turn(3, picked3, nc.scalar.copy)
-        v3_codes = sb.tile([P, P], U32, align_bytes=64)
-        v3_scales = sb.tile([P, P], U8, align_bytes=64)
-        quantize(nc, v3_codes[:], v3_scales[:], grouped3[:])
-        out3_ps = ps.tile([P, P], F32, tag="bank2")
-        product(nc, out3_ps[:], wt_codes[:], wt_scales[:], v3_codes[:], v3_scales[:])
-        tail = sb.tile([P, P], F32)
-        nc.scalar.copy(out=tail[:], in_=out3_ps[:])
-        nc.sync.dma_start(out=out[:, 3 * P :], in_=tail[:])
+        for b, grouped, copy in ((2, grouped2, nc.scalar.copy), (3, grouped3, nc.vector.tensor_copy)):
+            codes = sb.tile([P, P], U32, align_bytes=64, name="v_codes%d" % b)
+            scales = sb.tile([P, P], U8, align_bytes=64, name="v_scales%d" % b)
+            quantize(nc, codes[:], scales[:], grouped[:])
+            out_ps = ps.tile([P, P], F32, name="out_ps%d" % b, tag="bank%d" % (b - 1))
+            product(nc, out_ps[:], wt_codes[:], wt_scales[:], codes[:], scales[:])
+            result = sb.tile([P, P], F32, name="result%d" % b)
+            copy(out=result[:], in_=out_ps[:])
+            nc.sync.dma_start(out=out[:, b * P : (b + 1) * P], in_=result[:])

from contextlib import ExitStack

import concourse.mybir as mybir
from concourse.masks import make_identity

D, T, I, Q, E, Z = 512, 2048, 512, 128, 512, 1024
FLOPS = 2 * Q * (D * I + D * Z + I * E)

F32 = mybir.dt.float32
BF16 = mybir.dt.bfloat16
I32 = mybir.dt.int32
U32 = mybir.dt.uint32
U16 = mybir.dt.uint16
U8 = mybir.dt.uint8
FP8X4 = mybir.dt.float8_e4m3fn_x4
ALU = mybir.AluOpType
COPY = mybir.ActivationFunctionType.Copy

P = 128
PACK = 4
BANK = 512
LIST_COLS = I // 16
E_BLOCKS = E // P
LAST_VECTOR_COLS = 18


def interleave(copy, grouped, raw):
    copy(
        out=grouped.rearrange("p (c i) t -> p c t i", i=PACK),
        in_=raw.rearrange("p t (c i) -> p c t i", i=PACK),
    )


def quantize(nc, codes, scales, grouped):
    nc.vector.quantize_mx(out=codes.bitcast(FP8X4), scales=scales, in_=grouped.rearrange("p c t -> p (c t)"))


def product(nc, acc, lhs_codes, lhs_scales, rhs_codes, rhs_scales):
    nc.tensor.matmul_mx(
        out=acc,
        lhsT=lhs_codes.bitcast(FP8X4),
        lhsT_scale=lhs_scales,
        rhs=rhs_codes.bitcast(FP8X4),
        rhs_scale=rhs_scales,
        start=True,
        stop=True,
    )


def tile_attend_widelarger_read_lean_kernel(tc, query, query2, keys_words, keys_scales, pages, factors, vals, offs, offs2, out):
    nc = tc.nc
    with ExitStack() as ctx:
        sb = ctx.enter_context(tc.tile_pool(name="sb", bufs=1))
        ps = ctx.enter_context(tc.psum_pool(name="ps", bufs=1))

        token_list = sb.tile([P, LIST_COLS], U16)
        page_list = sb.tile([P, LIST_COLS], U16)
        pages_raw = [sb.tile([P, 2, Z], F32, name="pages_raw%d" % h) for h in range(2)]
        q2_raw = sb.tile([P, PACK, Q], F32)
        q_raw = sb.tile([P, PACK, Q], F32)
        slot_factor = sb.tile([P, PACK], F32)
        key_words = sb.tile([P, T], U32)
        key_bytes = sb.tile([P, T], U8)
        vals_raw = [sb.tile([P, T], F32, name="vals_raw%d" % b, tag="vals_raw%d" % b, align_bytes=64) for b in range(E_BLOCKS)]
        identity = sb.tile([P, P], F32)

        nc.gpsimd.memset(key_bytes[:].bitcast(I32), 0)
        scale_rows = keys_scales[0].rearrange("(g j) c -> j g c", j=PACK)
        for j in range(PACK):
            nc.gpsimd.dma_start(out=key_bytes[j:P:32, :].bitcast(I32), in_=scale_rows[j].bitcast(I32))
        nc.vector.memset(identity[:], 0.0)
        make_identity(nc, identity[:], nomemset=True)

        page_rows = pages.rearrange("(p t) z -> p t z", t=PACK)
        for h in range(2):
            nc.sync.dma_start(out=pages_raw[h][:], in_=page_rows[:, 2 * h : 2 * h + 2, :])
        nc.sync.dma_start(token_list[:], offs)
        nc.sync.dma_start(out=q2_raw[:], in_=query2.rearrange("(p t) q -> p t q", t=PACK))
        nc.sync.dma_start(out=q_raw[:], in_=query.rearrange("(p t) q -> p t q", t=PACK))
        nc.sync.dma_start(
            out=key_words[:].bitcast(I32), in_=keys_words[0].rearrange("p c r -> p (c r)").bitcast(I32)
        )
        nc.sync.dma_start(page_list[:], offs2)
        nc.sync.dma_start(out=slot_factor[:], in_=factors.rearrange("o (p t) -> p (o t)", t=PACK))
        for b in range(E_BLOCKS):
            nc.sync.dma_start(out=vals_raw[b][:], in_=vals[b * P : (b + 1) * P, :])

        pg_codes = sb.tile([P, Z], U32, align_bytes=64)
        pg_scales = sb.tile([P, Z], U8, align_bytes=64)
        q2_codes = sb.tile([P, Q], U32, align_bytes=64)
        q2_scales = sb.tile([P, Q], U8, align_bytes=64)
        q_codes = sb.tile([P, Q], U32, align_bytes=64)
        q_scales = sb.tile([P, Q], U8, align_bytes=64)
        pg_a = sb.tile([P, 512, PACK], BF16, align_bytes=64, tag="pg_a")
        pg_b = sb.tile([P, 512, PACK], BF16, align_bytes=64, tag="pg_b")
        q2_grouped = sb.tile([P, Q, PACK], BF16, align_bytes=64)
        q_grouped = sb.tile([P, Q, PACK], BF16, align_bytes=64)

        h0 = sb.tile([P, Z], F32, tag="h0", align_bytes=64)
        h0_ps = [ps.tile([P, BANK], F32, name="h0_ps%d" % n, tag="bank%d" % n) for n in range(Z // BANK)]

        def pair(copy, grouped, h, first, last):
            base = first // BANK * BANK
            copy(
                out=grouped[:, first - base : last - base, 2 * h : 2 * h + 2],
                in_=pages_raw[h][:, :, first:last].rearrange("p t z -> p z t"),
            )

        pair(nc.vector.tensor_copy, pg_a, 0, 0, 512)
        pair(nc.vector.tensor_copy, pg_b, 0, 512, 1024)
        pair(nc.vector.tensor_copy, pg_a, 1, 0, 512)
        pair(nc.scalar.copy, pg_b, 1, 768, 1024)
        pair(nc.vector.tensor_copy, pg_b, 1, 512, 768)
        interleave(nc.scalar.copy, q2_grouped[:], q2_raw[:])
        interleave(nc.scalar.copy, q_grouped[:], q_raw[:])
        quantize(nc, pg_codes[:, 0:512], pg_scales[:, 0:512], pg_a[:])
        quantize(nc, q2_codes[:], q2_scales[:], q2_grouped[:])
        quantize(nc, pg_codes[:, 512:1024], pg_scales[:, 512:1024], pg_b[:])
        quantize(nc, q_codes[:], q_scales[:], q_grouped[:])
        for n in range(Z // BANK):
            cols = slice(n * BANK, (n + 1) * BANK)
            product(nc, h0_ps[n][:], q2_codes[:], q2_scales[:], pg_codes[:, cols], pg_scales[:, cols])
            nc.scalar.copy(out=h0[:, cols], in_=h0_ps[n][:])

        picked_words = sb.tile([P, I], U32, align_bytes=64, tag="pg_a")
        picked_bytes = sb.tile([P, I], U8, align_bytes=64, tag="pg_b")
        nc.vector.tensor_copy(picked_bytes[:], key_bytes[:].indirect(token_list[:]))
        nc.vector.tensor_copy(picked_words[:], key_words[:].indirect(token_list[:]))
        a_ps = ps.tile([P, I], F32, tag="bank2")
        product(nc, a_ps[:], q_codes[:], q_scales[:], picked_words[:], picked_bytes[:])

        h0_picked = sb.tile([P, I], F32)
        nc.scalar.activation(h0_picked[:], h0[:].indirect(page_list[:]), COPY)
        weight = sb.tile([P, I], F32)
        nc.vector.scalar_tensor_tensor(
            out=weight[:], in0=a_ps[:], scalar=0.0, in1=h0_picked[:], op0=ALU.max, op1=ALU.max
        )
        wt_ps = ps.tile([P, PACK, Q], F32)
        for t in range(PACK):
            nc.tensor.transpose(wt_ps[:, t, :], weight[:, t:I:PACK], identity[:])
        wt_grouped = sb.tile([P, Q, PACK], BF16, align_bytes=64)
        nc.vector.tensor_tensor(
            out=wt_grouped[:],
            in0=wt_ps[:].rearrange("p t q -> p q t"),
            in1=slot_factor[:].unsqueeze(1).to_broadcast([P, Q, PACK]),
            op=ALU.mult,
        )
        wt_codes = sb.tile([P, Q], U32, align_bytes=64)
        wt_scales = sb.tile([P, Q], U8, align_bytes=64)
        quantize(nc, wt_codes[:], wt_scales[:], wt_grouped[:])

        def gather(b, cut):
            picked = sb.tile([P, I], BF16, name="picked%d" % b, tag=["h0", "picked1", "picked2", "picked3"][b], align_bytes=64)
            if cut > 0:
                nc.vector.tensor_copy(picked[:, : 16 * cut], vals_raw[b][:].indirect(token_list[:, :cut]))
            nc.scalar.activation(picked[:, 16 * cut :], vals_raw[b][:].indirect(token_list[:, cut:]), COPY)
            return picked

        def turn(b, picked, copy):
            pairs = picked[:].bitcast(F32)
            vt_ps = ps.tile([P, 2, P], F32, name="vt_ps%d" % b, tag=["bank2", "bank4", "bank5", "bank6"][b])
            for u in range(2):
                nc.tensor.transpose(vt_ps[:, u, :], pairs[:, u : I // 2 : 2], identity[:])
            vt_grouped = sb.tile([P, P, PACK], BF16, align_bytes=64, name="vt_grouped%d" % b, tag=["vt0", "vt1", "vals_raw3", "vt3"][b])
            copy(out=vt_grouped[:].bitcast(F32), in_=vt_ps[:].rearrange("p u e -> p e u"))
            return vt_grouped

        v01_codes = sb.tile([P, 2 * P], U32, align_bytes=64)
        v01_scales = sb.tile([P, 2 * P], U8, align_bytes=64)
        for b in range(2):
            grouped = turn(b, gather(b, 0), nc.vector.tensor_copy)
            quantize(nc, v01_codes[:, b * P : (b + 1) * P], v01_scales[:, b * P : (b + 1) * P], grouped[:])
        out01_ps = ps.tile([P, 2 * P], F32, tag="bank0")
        product(nc, out01_ps[:], wt_codes[:], wt_scales[:], v01_codes[:], v01_scales[:])
        head = sb.tile([P, 2 * P], F32)
        nc.vector.tensor_copy(out=head[:], in_=out01_ps[:])
        nc.sync.dma_start(out=out[:, : 2 * P], in_=head[:])
        picked2 = gather(2, 0)
        picked3 = gather(3, LAST_VECTOR_COLS)
        grouped2 = turn(2, picked2, nc.scalar.copy)
        grouped3 = turn(3, picked3, nc.scalar.copy)
        for b, grouped, copy in ((2, grouped2, nc.scalar.copy), (3, grouped3, nc.vector.tensor_copy)):
            codes = sb.tile([P, P], U32, align_bytes=64, name="v_codes%d" % b)
            scales = sb.tile([P, P], U8, align_bytes=64, name="v_scales%d" % b)
            quantize(nc, codes[:], scales[:], grouped[:])
            out_ps = ps.tile([P, P], F32, name="out_ps%d" % b, tag="bank%d" % (b - 1))
            product(nc, out_ps[:], wt_codes[:], wt_scales[:], codes[:], scales[:])
            result = sb.tile([P, P], F32, name="result%d" % b)
            copy(out=result[:], in_=out_ps[:])
            nc.sync.dma_start(out=out[:, b * P : (b + 1) * P], in_=result[:])
